import numpy as np
import ml_dtypes


def mxq(x, axis, fmt="e4m3"):
    dtype, down = {"e4m3": (ml_dtypes.float8_e4m3fn, 7), "e5m2": (ml_dtypes.float8_e5m2, 14)}[fmt]
    v = np.moveaxis(np.asarray(x, np.float32).astype(ml_dtypes.bfloat16).astype(np.float64), axis, -1)
    blocks = v.reshape(v.shape[:-1] + (-1, 32))
    amax = np.abs(blocks).max(-1, keepdims=True)
    byte = np.maximum(np.where(amax > 0, np.frexp(amax)[1] - 1 + 127, 0) - down, 1)
    scale = np.exp2(byte - 127.0)
    codes = (blocks / scale).astype(np.float32).astype(dtype).astype(np.float64)
    return np.moveaxis((codes * scale).reshape(v.shape), -1, axis)


WIDE = False


def mx_kscale(k):
    if not WIDE:
        return np.ones(k)
    levels = np.array([10, -10, 5, -5, 0])
    if k % 512:
        return np.exp2(np.random.permutation(np.resize(levels, k // 32))).repeat(32)
    a = np.empty((k // 512, 16))
    for p in range(k // 512):
        a[p, :8] = np.random.permutation(np.resize(levels, 8))
        for g in range(8):
            far = levels[np.abs(levels - a[p, g]) >= 10]
            a[p, g + 8] = far[np.random.randint(len(far))]
    return np.exp2(a.ravel()).repeat(32)


def f64(x):
    return np.asarray(x).astype(np.float64)


def striped(idx):
    return np.tile(idx.reshape(-1, 16).T, (8, 1)).astype(np.uint16)


def unstriped(offs):
    return offs[:16].T.reshape(-1).astype(np.int64)


def pack_weight(w):
    k, n = w.shape
    w = f64(np.asarray(w, np.float32).astype(ml_dtypes.bfloat16)).reshape(k // 32, 32, n)
    amax = np.abs(w).max(1)
    byte = np.clip(np.where(amax > 0, np.frexp(amax)[1] - 1 + 127 - 7, 1), 1, 254)
    scaled = (w * np.exp2(127.0 - byte)[:, None, :]).reshape(k, n).astype(np.float32)
    words = np.ascontiguousarray(scaled.reshape(k // 512, 128, 4, n).transpose(0, 1, 3, 2)).astype(ml_dtypes.float8_e4m3fn).view(np.uint8)
    return words, np.ascontiguousarray(byte.astype(np.uint8).reshape(k // 512, 16, n))


def unpack_weight(words, scales):
    g, p, n, _ = words.shape
    vals = np.ascontiguousarray(words).view(ml_dtypes.float8_e4m3fn).astype(np.float64) * np.repeat(np.exp2(scales.astype(np.float64) - 127.0), 8, axis=1)[..., None]
    return vals.transpose(0, 1, 3, 2).reshape(g * 512, n)


def sigmoid(v):
    return 1.0 / (1.0 + np.exp(-np.maximum(v, -700.0)))


K, T, S, D, N, H = 1024, 2048, 1024, 4, 128, 512


def setup_inputs():
    n = np.random.standard_normal
    s = mx_kscale(K)[:, None]
    u = mx_kscale(H)
    packed_xT = pack_weight(n((K, T)) * s)
    return {
        "x_words": packed_xT[0],
        "x_scales": packed_xT[1],
        "w1": (n((K, H)) / np.sqrt(K) / s).astype(np.float32),
        "w2": (n((K, H)) / np.sqrt(K) / s).astype(np.float32),
        "unit": (np.random.uniform(0.6, 1.4, (H, 1)) * u[:, None]).astype(np.float32),
        "w3": (n((H, N)) / np.sqrt(H) / u[:, None]).astype(np.float32),
        "offs": striped(np.random.permutation(T)[:S]),
        "adv": striped(np.random.permutation(S)),
    }


def reference(x_words, x_scales, w1, w2, unit, w3, offs, adv):
    xq = unpack_weight(x_words, x_scales)[:, unstriped(offs)]
    y = mxq(f64(w1), 0, "e4m3").T @ xq
    ctr = sigmoid(y)
    yp = mxq(f64(w2), 0, "e4m3").T @ xq
    bid = np.log(np.exp(yp) + 1.0)
    ecpm = ctr * bid
    win = ecpm.reshape(len(ecpm), -1, D).max(axis=2)
    soft = np.exp(2.0 * (np.tanh(ecpm - np.repeat(win, D, axis=1))))
    sum4 = ecpm.reshape(len(ecpm), -1, D).sum(axis=2) + 0.2
    pay = (soft * (np.repeat(sum4, D, axis=1) - ecpm)) / (ctr + 0.3)
    pa = pay[:, unstriped(adv)]
    hid = f64(unit) * (pay - (0.4 * pa))
    return mxq(f64(w3), 0, "e4m3").T @ mxq(hid, 0, "e4m3")

@@ -1,0 +1,281 @@
+import math
+from contextlib import ExitStack
+
+import concourse.mybir as mybir
+from concourse.masks import make_identity
+
+K, T, S, D, N, H = 1024, 2048, 1024, 4, 128, 512
+FLOPS = 2 * (2 * K * H * S + H * N * S)
+
+F32 = mybir.dt.float32
+BF16 = mybir.dt.bfloat16
+I32 = mybir.dt.int32
+U32 = mybir.dt.uint32
+U16 = mybir.dt.uint16
+U8 = mybir.dt.uint8
+FP8X4 = mybir.dt.float8_e4m3fn_x4
+ALU = mybir.AluOpType
+ACT = mybir.ActivationFunctionType
+
+P = 128
+PACK = 4
+K_PASS = P * PACK
+PASSES = K // K_PASS
+BANK = 512
+BLOCKS = S // BANK
+TAIL = 256
+SOFTPLUS_CAP = 40.0
+ORDER = (0, 1)
+EDGE = 16
+ON_VECTOR = (1,)
+LOG_CUTS = ((0, 1024), (1024, 2048), (2048, 3072), (3072, 4096))
+
+
+def tile_picked_yhqads_pay_p_kernel(tc, x_words, x_scales, w1, w2, unit, w3, offs, adv, out):
+    nc = tc.nc
+    with ExitStack() as ctx:
+        keep = ctx.enter_context(tc.tile_pool(name="keep", bufs=1))
+        work = ctx.enter_context(tc.tile_pool(name="work", bufs=2))
+        ring = ctx.enter_context(tc.tile_pool(name="ring", bufs=4))
+        psum = ctx.enter_context(tc.psum_pool(name="psum", bufs=1))
+
+        offs_sb = keep.tile([P, S // 16], U16, name="offs_sb")
+        adv_sb = keep.tile([P, S // 16], U16, name="adv_sb")
+        table_scales = keep.tile([P, T], U8, name="table_scales", align_bytes=64)
+        scale_rows = keep.tile([P, T // 4], I32, name="scale_rows", align_bytes=64)
+        table_words = [keep.tile([P, T], I32, name=f"table_words{o}", align_bytes=64) for o in range(PASSES)]
+        w_raw = {}
+        for nm in ("w2", "w1"):
+            for o in range(PASSES):
+                w_raw[nm, o] = keep.tile([P, PACK, H], F32, name=f"{nm}_raw{o}", align_bytes=64)
+        w3_raw = keep.tile([P, PACK, N], F32, name="w3_raw", align_bytes=64)
+        unit_sb = keep.tile([P, PACK], F32, name="unit_sb")
+
+        def load_weight(nm, w, o):
+            rows = w[o * K_PASS : (o + 1) * K_PASS, :]
+            nc.sync.dma_start(out=w_raw[nm, o][:], in_=rows.rearrange("(p j) c -> p j c", j=PACK))
+
+        def load_words(o):
+            nc.sync.dma_start(out=table_words[o][:], in_=x_words[o].rearrange("p n t -> p (n t)").bitcast(I32))
+
+        nc.vector.memset(table_scales[:].bitcast(I32), 0)
+        nc.sync.dma_start(offs_sb[:], offs)
+        for q in range(4):
+            nc.sync.dma_start(
+                out=scale_rows[32 * q : 32 * q + 4 * PASSES, :],
+                in_=x_scales[:, 4 * q : 4 * q + 4, :].bitcast(I32),
+            )
+        load_weight("w2", w2, 0)
+        load_words(0)
+        load_words(1)
+        load_weight("w2", w2, 1)
+        load_weight("w1", w1, 0)
+        load_weight("w1", w1, 1)
+        nc.sync.dma_start(adv_sb[:], adv)
+        nc.sync.dma_start(out=unit_sb[:], in_=unit.rearrange("(p t) o -> p (t o)", t=PACK))
+        nc.sync.dma_start(out=w3_raw[:], in_=w3.rearrange("(p j) n -> p j n", j=PACK))
+
+        ident = keep.tile([P, P], F32, name="ident")
+        make_identity(nc, ident[:])
+        picked_sc = keep.tile([P, S], U8, name="picked_sc", align_bytes=64)
+        x_sc = keep.tile([P, BLOCKS, D, P], U8, name="x_sc", align_bytes=64)
+        x_codes = {}
+        w_codes = {}
+        w_sc = {}
+        w_bf = {}
+        for key in w_raw:
+            w_bf[key] = keep.tile([P, PACK, P, PACK], BF16, name=f"{key[0]}_bf{key[1]}", align_bytes=64)
+            w_codes[key] = keep.tile([P, H], U32, name=f"{key[0]}_codes{key[1]}", align_bytes=64)
+            w_sc[key] = keep.tile([P, H], U8, name=f"{key[0]}_sc{key[1]}", align_bytes=64)
+
+        def gather_words(o, b):
+            tag = "w2_bf1" if (o, b) == (1, 1) else f"x_codes{o}{b}"
+            x_codes[o, b] = keep.tile([P, D, P], U32, name=f"x_codes{o}{b}", tag=tag, align_bytes=64)
+            nc.vector.tensor_copy(
+                out=x_codes[o, b][:].rearrange("p d v -> p v d"),
+                in_=table_words[o][:].bitcast(U32).indirect(offs_sb[:, b * BANK // 16 : (b + 1) * BANK // 16]),
+            )
+
+        def round_weight(key, on_scalar):
+            dst = w_bf[key][:].rearrange("p t m j -> p m j t")
+            src = w_raw[key][:].rearrange("p j (m t) -> p m j t", t=PACK)
+            if on_scalar > 0:
+                nc.scalar.copy(out=dst[:, :on_scalar], in_=src[:, :on_scalar])
+            if on_scalar < P:
+                nc.vector.tensor_copy(out=dst[:, on_scalar:], in_=src[:, on_scalar:])
+
+        def quantize_weight(key):
+            nc.vector.quantize_mx(
+                out=w_codes[key][:].bitcast(FP8X4),
+                scales=w_sc[key][:],
+                in_=w_bf[key][:].rearrange("p t m j -> p (t m j)"),
+            )
+
+        def product(nm, b, d):
+            acc = psum.tile([P, BANK], F32, name=f"bank{D * ORDER.index(b) + d}")
+            for o in range(PASSES):
+                nc.tensor.matmul_mx(
+                    out=acc[:],
+                    lhsT=x_codes[o, b][:, d, :].bitcast(FP8X4),
+                    lhsT_scale=x_sc[4 * o :, b, d, :],
+                    rhs=w_codes[nm, o][:].bitcast(FP8X4),
+                    rhs_scale=w_sc[nm, o][:],
+                    start=(o == 0),
+                    stop=(o == PASSES - 1),
+                )
+            return acc
+
+        for q in range(4):
+            live = slice(32 * q, 32 * q + 4 * PASSES)
+            nc.vector.tensor_copy(out=table_scales[live, :].bitcast(I32), in_=scale_rows[live, :])
+
+        def gather_scales(b):
+            picked = picked_sc[:, b * BANK : (b + 1) * BANK]
+            nc.vector.tensor_copy(out=picked, in_=table_scales[:].indirect(offs_sb[:, b * BANK // 16 : (b + 1) * BANK // 16]))
+            nc.vector.tensor_copy(out=x_sc[:, b].rearrange("p d v -> p v d"), in_=picked.rearrange("p (v d) -> p v d", d=D))
+
+        gather_scales(0)
+        round_weight(("w2", 0), P)
+        quantize_weight(("w2", 0))
+        gather_words(0, 0)
+        gather_words(1, 0)
+        round_weight(("w2", 1), 56)
+        quantize_weight(("w2", 1))
+        gather_scales(1)
+        gather_words(0, 1)
+        gather_words(1, 1)
+
+        logs = keep.tile([P, BLOCKS, D, H], F32, name="logs")
+        pay = keep.tile([P, PACK, S], F32, name="pay")
+        pay_adv = keep.tile([P, PACK, S], F32, name="pay_adv")
+        row_factor = keep.tile([P, PACK], F32, name="row_factor")
+        yp = {}
+        for b in range(BLOCKS):
+            for d in range(D):
+                yp[b, d] = product("w2", b, d)
+                nc.scalar.activation(logs[:, b, d, :], yp[b, d][:], ACT.Exp)
+        flat_logs = logs[:].rearrange("p b d c -> p (b d c)")
+        by_bank = logs[:].rearrange("p b d c -> p (b d) c")
+        for piece in [by_bank[:, n : n + 2, EDGE:] for n in range(0, BLOCKS * D, 2)] + [by_bank[:, :, :EDGE]]:
+            nc.vector.tensor_scalar(piece, piece, math.exp(SOFTPLUS_CAP), None, ALU.min)
+        round_weight(("w1", 0), 0)
+        quantize_weight(("w1", 0))
+        round_weight(("w1", 1), 0)
+        quantize_weight(("w1", 1))
+        for lo, hi in LOG_CUTS:
+            nc.scalar.activation(flat_logs[:, lo:hi], flat_logs[:, lo:hi], ACT.Ln, bias=1.0)
+        nc.vector.tensor_scalar(row_factor[:], unit_sb[:], -25.0 / 39.0, None, ALU.mult)
+        for b in ORDER:
+            for d in range(D):
+                nc.vector.tensor_tensor(logs[:, b, d, :], yp[b, d][:], logs[:, b, d, :], ALU.max)
+
+        turns = []
+
+        def values(b):
+            half_tanh = work.tile([P, D, H], F32, name="ecpm2")
+            shift_tanh = work.tile([P, D, H], F32, name="shift_tanh")
+            ys = [product("w1", b, d) for d in range(D)]
+            for d in range(D):
+                nc.scalar.activation(half_tanh[:, d, :], ys[d][:], ACT.Tanh, scale=0.5)
+            for d in range(D):
+                nc.scalar.activation(shift_tanh[:, d, :], ys[d][:], ACT.Tanh, scale=0.5, bias=0.5 * math.log(1.3 / 0.3))
+            ecpm2 = half_tanh
+            for h in range(2):
+                pair = slice(2 * h, 2 * h + 2)
+                nc.vector.scalar_tensor_tensor(ecpm2[:, pair, :], half_tanh[:, pair, :], 1.0, logs[:, b, pair, :], ALU.add, ALU.mult)
+            pair_max = work.tile([P, 2, H], F32, name="pair_max")
+            nc.vector.tensor_tensor(pair_max[:], ecpm2[:, 0:2, :], ecpm2[:, 2:4, :], ALU.max)
+            pair_sum = work.tile([P, 2, H], F32, name="pair_sum")
+            neg_win2 = work.tile([P, H], F32, name="neg_win2")
+            nc.vector.scalar_tensor_tensor(pair_sum[:, 0, :], ecpm2[:, 0, :], 0.4, ecpm2[:, 1, :], ALU.add, ALU.add)
+            nc.vector.tensor_tensor(neg_win2[:], pair_max[:, 0, :], pair_max[:, 1, :], ALU.max)
+            nc.vector.scalar_tensor_tensor(pair_sum[:, 1, :], ecpm2[:, 2, :], 0.4, ecpm2[:, 3, :], ALU.add, ALU.add)
+            nc.vector.tensor_scalar(neg_win2[:], neg_win2[:], -1.0, None, ALU.mult)
+            return ecpm2, pair_sum, neg_win2, shift_tanh
+
+        def turned_sum(terms):
+            acc = psum.tile([P, D, P], F32, name=f"bank{len(turns) % 8}")
+            turns.append(acc)
+            for d in range(D):
+                for n, term in enumerate(terms[d]):
+                    nc.tensor.matmul(
+                        acc[:, d, :], term, ident[:], start=(n == 0), stop=(n == len(terms[d]) - 1), is_transpose=True
+                    )
+            return acc[:].rearrange("p d v -> p v d")
+
+        def auction(b, t, ecpm2, pair_sum, neg_win2, shift_tanh):
+            rows = slice(t * P, (t + 1) * P)
+            gap2 = turned_sum([[neg_win2[:, rows], ecpm2[:, d, rows]] for d in range(D)])
+            others2 = turned_sum([[pair_sum[:, 1 - d // 2, rows], ecpm2[:, d ^ 1, rows]] for d in range(D)])
+            shift_turned = turned_sum([[shift_tanh[:, d, rows]] for d in range(D)])
+            soft = ring.tile([P, P, D], F32, name="soft")
+            nc.scalar.activation(soft[:], gap2, ACT.Tanh, scale=0.5)
+            nc.scalar.activation(soft[:], soft[:], ACT.Exp, scale=2.0)
+            price = ring.tile([P, P, D], F32, name="price")
+            nc.vector.scalar_tensor_tensor(price[:], others2, row_factor[:, t : t + 1], soft[:], ALU.mult, ALU.mult)
+            nc.vector.scalar_tensor_tensor(
+                pay[:, t, b * BANK : (b + 1) * BANK].rearrange("p (v d) -> p v d", d=D),
+                shift_turned,
+                1.6,
+                price[:],
+                ALU.subtract,
+                ALU.mult,
+            )
+
+        def fetch_adv(t, a):
+            if t in ON_VECTOR:
+                nc.vector.tensor_copy(
+                    out=pay_adv[:, t, a : a + TAIL], in_=scaled[t][:].indirect(adv_sb[:, a // 16 : (a + TAIL) // 16])
+                )
+                return
+            nc.scalar.activation(
+                pay_adv[:, t, a : a + TAIL],
+                pay[:, t, :].indirect(adv_sb[:, a // 16 : (a + TAIL) // 16]),
+                ACT.Copy,
+                scale=-0.4,
+            )
+
+        made = {b: values(b) for b in ORDER}
+        w3_bf = keep.tile([P, N, PACK], BF16, name="w3_bf", align_bytes=64)
+        w3_codes = keep.tile([P, N], U32, name="w3_codes", align_bytes=64)
+        w3_sc = keep.tile([P, N], U8, name="w3_sc", align_bytes=64)
+        nc.vector.tensor_copy(out=w3_bf[:], in_=w3_raw[:].rearrange("p j n -> p n j"))
+        nc.vector.quantize_mx(out=w3_codes[:].bitcast(FP8X4), scales=w3_sc[:], in_=w3_bf[:].rearrange("p n j -> p (n j)"))
+
+        for b in ORDER:
+            for t in range(PACK):
+                auction(b, t, *made[b])
+        scaled = {}
+        for t in ON_VECTOR:
+            scaled[t] = keep.tile([P, S], F32, name=f"scaled{t}")
+            nc.vector.tensor_scalar(scaled[t][:], pay[:, t, :], -0.4, None, ALU.mult)
+
+        for a in range(0, S, TAIL):
+            cols = slice(a, a + TAIL)
+            for t in range(PACK):
+                fetch_adv(t, a)
+            hid_bf = ring.tile([P, TAIL, PACK], BF16, name="hid_bf", align_bytes=64)
+            nc.vector.tensor_tensor(
+                hid_bf[:].rearrange("p (c i) t -> p c t i", i=4),
+                pay[:, :, cols].rearrange("p t (c i) -> p c t i", i=4),
+                pay_adv[:, :, cols].rearrange("p t (c i) -> p c t i", i=4),
+                ALU.add,
+            )
+            hid_codes = ring.tile([P, TAIL], U32, name="hid_codes", align_bytes=64)
+            hid_sc = ring.tile([P, TAIL], U8, name="hid_sc", align_bytes=64)
+            nc.vector.quantize_mx(
+                out=hid_codes[:].bitcast(FP8X4), scales=hid_sc[:], in_=hid_bf[:].rearrange("p c t -> p (c t)")
+            )
+            acc = psum.tile([P, BANK], F32, name=f"bank{a // TAIL}")
+            nc.tensor.matmul_mx(
+                out=acc[:, :TAIL],
+                lhsT=w3_codes[:].bitcast(FP8X4),
+                lhsT_scale=w3_sc[:],
+                rhs=hid_codes[:].bitcast(FP8X4),
+                rhs_scale=hid_sc[:],
+                start=True,
+                stop=True,
+            )
+            result = ring.tile([P, TAIL], F32, name="result")
+            nc.scalar.copy(out=result[:], in_=acc[:, :TAIL])
+            nc.sync.dma_start(out=out[:, cols], in_=result[:])

@@ -23,12 +23,17 @@ K_PASS = P * PACK
 PASSES = K // K_PASS
 BANK = 512
 BLOCKS = S // BANK
-TAIL = 256
+CHUNKS = ((0, 256), (256, 256), (512, 256), (768, 128), (896, 128))
 SOFTPLUS_CAP = 40.0
-ORDER = (0, 1)
+SHIFT = 0.5 * math.log(1.3 / 0.3)
 EDGE = 16
-ON_VECTOR = (1,)
-LOG_CUTS = ((0, 1024), (1024, 2048), (2048, 3072), (3072, 4096))
+PAIRED = (0, 1)
+CUTS = 4
+SHARE = 48
+ON_VECTOR = ()
+TURNED = 2
+WIDE = TURNED * P
+PLAN = "A0 A1 N002 U02 U12 N102 U03 U13"
 
 
 def tile_picked_yhqads_pay_p_kernel(tc, x_words, x_scales, w1, w2, unit, w3, offs, adv, out):
@@ -36,7 +41,8 @@ def tile_picked_yhqads_pay_p_kernel(tc, x_words, x_scales, w1, w2, unit, w3, off
     with ExitStack() as ctx:
         keep = ctx.enter_context(tc.tile_pool(name="keep", bufs=1))
         work = ctx.enter_context(tc.tile_pool(name="work", bufs=2))
-        ring = ctx.enter_context(tc.tile_pool(name="ring", bufs=4))
+        ring = ctx.enter_context(tc.tile_pool(name="ring", bufs=3))
+        last = ctx.enter_context(tc.tile_pool(name="last", bufs=4))
         psum = ctx.enter_context(tc.psum_pool(name="psum", bufs=1))
 
         offs_sb = keep.tile([P, S // 16], U16, name="offs_sb")
@@ -101,7 +107,10 @@ def tile_picked_yhqads_pay_p_kernel(tc, x_words, x_scales, w1, w2, unit, w3, off
             src = w_raw[key][:].rearrange("p j (m t) -> p m j t", t=PACK)
             if on_scalar > 0:
                 nc.scalar.copy(out=dst[:, :on_scalar], in_=src[:, :on_scalar])
-            if on_scalar < P:
+            if on_scalar == 0:
+                for m in range(0, P, P // CUTS):
+                    nc.vector.tensor_copy(out=dst[:, m : m + P // CUTS], in_=src[:, m : m + P // CUTS])
+            elif on_scalar < P:
                 nc.vector.tensor_copy(out=dst[:, on_scalar:], in_=src[:, on_scalar:])
 
         def quantize_weight(key):
@@ -111,19 +120,36 @@ def tile_picked_yhqads_pay_p_kernel(tc, x_words, x_scales, w1, w2, unit, w3, off
                 in_=w_bf[key][:].rearrange("p t m j -> p (t m j)"),
             )
 
-        def product(nm, b, d):
-            acc = psum.tile([P, BANK], F32, name=f"bank{D * ORDER.index(b) + d}")
+        def product(nm, bank):
+            acc = psum.tile([P, BANK], F32, name=f"bank{bank}")
+            if bank < 4:
+                b, pair = divmod(bank, 2)
+                for o in range(PASSES):
+                    for e in range(2):
+                        d = 2 * pair + e
+                        nc.tensor.matmul_mx(
+                            out=acc[:, e * WIDE : (e + 1) * WIDE],
+                            lhsT=x_codes[o, b][:, d, :].bitcast(FP8X4),
+                            lhsT_scale=x_sc[4 * o :, b, d, :],
+                            rhs=w_codes[nm, o][:, H - WIDE :].bitcast(FP8X4),
+                            rhs_scale=w_sc[nm, o][:, H - WIDE :],
+                            start=(o == 0 and e == 0),
+                            stop=(o == PASSES - 1 and e == 1),
+                        )
+                return acc[:].rearrange("p (v d) -> p v d", d=D)
+            t, b = divmod(bank - 4, 2)
+            rows = slice(t * P, (t + 1) * P)
             for o in range(PASSES):
                 nc.tensor.matmul_mx(
                     out=acc[:],
-                    lhsT=x_codes[o, b][:, d, :].bitcast(FP8X4),
-                    lhsT_scale=x_sc[4 * o :, b, d, :],
-                    rhs=w_codes[nm, o][:].bitcast(FP8X4),
-                    rhs_scale=w_sc[nm, o][:],
+                    lhsT=w_codes[nm, o][:, rows].bitcast(FP8X4),
+                    lhsT_scale=w_sc[nm, o][:, rows],
+                    rhs=x_codes[o, b][:].rearrange("p d v -> p (d v)").bitcast(FP8X4),
+                    rhs_scale=x_sc[4 * o :, b].rearrange("p d v -> p (d v)"),
                     start=(o == 0),
                     stop=(o == PASSES - 1),
                 )
-            return acc
+            return acc[:].rearrange("p (d v) -> p v d", d=D)
 
         for q in range(4):
             live = slice(32 * q, 32 * q + 4 * PASSES)
@@ -139,75 +165,87 @@ def tile_picked_yhqads_pay_p_kernel(tc, x_words, x_scales, w1, w2, unit, w3, off
         quantize_weight(("w2", 0))
         gather_words(0, 0)
         gather_words(1, 0)
-        round_weight(("w2", 1), 56)
+        round_weight(("w2", 1), SHARE)
         quantize_weight(("w2", 1))
         gather_scales(1)
         gather_words(0, 1)
         gather_words(1, 1)
 
-        logs = keep.tile([P, BLOCKS, D, H], F32, name="logs")
+        logs = keep.tile([P, 8, BANK], F32, name="logs")
+        half_tanh = keep.tile([P, 8, BANK], F32, name="half_tanh")
+        shift_tanh = keep.tile([P, 8, BANK], F32, name="shift_tanh")
         pay = keep.tile([P, PACK, S], F32, name="pay")
         pay_adv = keep.tile([P, PACK, S], F32, name="pay_adv")
         row_factor = keep.tile([P, PACK], F32, name="row_factor")
+
+        def as_bank(tile, bank):
+            return tile[:, bank, :].rearrange("p (v d) -> p v d", d=D)
+
         yp = {}
-        for b in range(BLOCKS):
-            for d in range(D):
-                yp[b, d] = product("w2", b, d)
-                nc.scalar.activation(logs[:, b, d, :], yp[b, d][:], ACT.Exp)
-        flat_logs = logs[:].rearrange("p b d c -> p (b d c)")
-        by_bank = logs[:].rearrange("p b d c -> p (b d) c")
-        for piece in [by_bank[:, n : n + 2, EDGE:] for n in range(0, BLOCKS * D, 2)] + [by_bank[:, :, :EDGE]]:
+        for bank in (0, 1, 4, 6, 2, 3, 5, 7):
+            yp[bank] = product("w2", bank)
+            nc.scalar.activation(as_bank(logs, bank), yp[bank], ACT.Exp)
+        for piece in [logs[:, 0:2, EDGE:], logs[:, 4::2, EDGE:], logs[:, 2:4, EDGE:], logs[:, 5::2, EDGE:], logs[:, :, :EDGE]]:
             nc.vector.tensor_scalar(piece, piece, math.exp(SOFTPLUS_CAP), None, ALU.min)
         round_weight(("w1", 0), 0)
         quantize_weight(("w1", 0))
         round_weight(("w1", 1), 0)
         quantize_weight(("w1", 1))
-        for lo, hi in LOG_CUTS:
-            nc.scalar.activation(flat_logs[:, lo:hi], flat_logs[:, lo:hi], ACT.Ln, bias=1.0)
+        for n in range(0, 8, 2):
+            nc.scalar.activation(logs[:, n : n + 2, :], logs[:, n : n + 2, :], ACT.Ln, bias=1.0)
         nc.vector.tensor_scalar(row_factor[:], unit_sb[:], -25.0 / 39.0, None, ALU.mult)
-        for b in ORDER:
-            for d in range(D):
-                nc.vector.tensor_tensor(logs[:, b, d, :], yp[b, d][:], logs[:, b, d, :], ALU.max)
+        for bank in range(8):
+            nc.vector.tensor_tensor(as_bank(logs, bank), yp[bank], as_bank(logs, bank), ALU.max)
+        for banks in ((0, 1, 2, 3), (4, 5), (6, 7)):
+            ys = {bank: product("w1", bank) for bank in banks}
+            for bank in banks:
+                nc.scalar.activation(as_bank(half_tanh, bank), ys[bank], ACT.Tanh, scale=0.5)
+            for bank in banks:
+                nc.scalar.activation(as_bank(shift_tanh, bank), ys[bank], ACT.Tanh, scale=0.5, bias=SHIFT)
+
+        terms = {}
+
+        def group_terms(b):
+            ecpm2 = work.tile([P, D, WIDE], F32, name="ecpm2")
+            pair_max = work.tile([P, 2, WIDE], F32, name="pair_max")
+            pair_sum = work.tile([P, 2, WIDE], F32, name="pair_sum")
+            neg_win2 = work.tile([P, WIDE], F32, name="neg_win2")
+            for pair in range(2):
+                nc.vector.scalar_tensor_tensor(
+                    ecpm2[:, 2 * pair : 2 * pair + 2, :].rearrange("p e c -> p (e c)"),
+                    half_tanh[:, 2 * b + pair, :],
+                    1.0,
+                    logs[:, 2 * b + pair, :],
+                    ALU.add,
+                    ALU.mult,
+                )
+            nc.vector.tensor_tensor(pair_max[:], ecpm2[:, 0:2, :], ecpm2[:, 2:4, :], ALU.max)
+            if b in PAIRED:
+                nc.vector.scalar_tensor_tensor(pair_sum[:], ecpm2[:, 0::2, :], 0.4, ecpm2[:, 1::2, :], ALU.add, ALU.add)
+            nc.vector.tensor_tensor(neg_win2[:], pair_max[:, 0, :], pair_max[:, 1, :], ALU.max)
+            nc.vector.tensor_scalar(neg_win2[:], neg_win2[:], -1.0, None, ALU.mult)
+            terms[b] = ecpm2, pair_sum, neg_win2
 
         turns = []
 
-        def values(b):
-            half_tanh = work.tile([P, D, H], F32, name="ecpm2")
-            shift_tanh = work.tile([P, D, H], F32, name="shift_tanh")
-            ys = [product("w1", b, d) for d in range(D)]
-            for d in range(D):
-                nc.scalar.activation(half_tanh[:, d, :], ys[d][:], ACT.Tanh, scale=0.5)
-            for d in range(D):
-                nc.scalar.activation(shift_tanh[:, d, :], ys[d][:], ACT.Tanh, scale=0.5, bias=0.5 * math.log(1.3 / 0.3))
-            ecpm2 = half_tanh
-            for h in range(2):
-                pair = slice(2 * h, 2 * h + 2)
-                nc.vector.scalar_tensor_tensor(ecpm2[:, pair, :], half_tanh[:, pair, :], 1.0, logs[:, b, pair, :], ALU.add, ALU.mult)
-            pair_max = work.tile([P, 2, H], F32, name="pair_max")
-            nc.vector.tensor_tensor(pair_max[:], ecpm2[:, 0:2, :], ecpm2[:, 2:4, :], ALU.max)
-            pair_sum = work.tile([P, 2, H], F32, name="pair_sum")
-            neg_win2 = work.tile([P, H], F32, name="neg_win2")
-            nc.vector.scalar_tensor_tensor(pair_sum[:, 0, :], ecpm2[:, 0, :], 0.4, ecpm2[:, 1, :], ALU.add, ALU.add)
-            nc.vector.tensor_tensor(neg_win2[:], pair_max[:, 0, :], pair_max[:, 1, :], ALU.max)
-            nc.vector.scalar_tensor_tensor(pair_sum[:, 1, :], ecpm2[:, 2, :], 0.4, ecpm2[:, 3, :], ALU.add, ALU.add)
-            nc.vector.tensor_scalar(neg_win2[:], neg_win2[:], -1.0, None, ALU.mult)
-            return ecpm2, pair_sum, neg_win2, shift_tanh
-
-        def turned_sum(terms):
+        def turned_sum(parts):
             acc = psum.tile([P, D, P], F32, name=f"bank{len(turns) % 8}")
             turns.append(acc)
             for d in range(D):
-                for n, term in enumerate(terms[d]):
+                for n, part in enumerate(parts[d]):
                     nc.tensor.matmul(
-                        acc[:, d, :], term, ident[:], start=(n == 0), stop=(n == len(terms[d]) - 1), is_transpose=True
+                        acc[:, d, :], part, ident[:], start=(n == 0), stop=(n == len(parts[d]) - 1), is_transpose=True
                     )
             return acc[:].rearrange("p d v -> p v d")
 
-        def auction(b, t, ecpm2, pair_sum, neg_win2, shift_tanh):
-            rows = slice(t * P, (t + 1) * P)
-            gap2 = turned_sum([[neg_win2[:, rows], ecpm2[:, d, rows]] for d in range(D)])
+        def turned_auction(b, t):
+            ecpm2, pair_sum, neg_win2 = terms[b]
+            lo = (t - (PACK - TURNED)) * P
+            rows = slice(lo, lo + P)
+            shifted = shift_tanh[:, 2 * b : 2 * b + 2, :].rearrange("p a (e c) -> p (a e) c", e=2)
             others2 = turned_sum([[pair_sum[:, 1 - d // 2, rows], ecpm2[:, d ^ 1, rows]] for d in range(D)])
-            shift_turned = turned_sum([[shift_tanh[:, d, rows]] for d in range(D)])
+            gap2 = turned_sum([[neg_win2[:, rows], ecpm2[:, d, rows]] for d in range(D)])
+            shift_turned = turned_sum([[shifted[:, d, rows]] for d in range(D)])
             soft = ring.tile([P, P, D], F32, name="soft")
             nc.scalar.activation(soft[:], gap2, ACT.Tanh, scale=0.5)
             nc.scalar.activation(soft[:], soft[:], ACT.Exp, scale=2.0)
@@ -222,7 +260,49 @@ def tile_picked_yhqads_pay_p_kernel(tc, x_words, x_scales, w1, w2, unit, w3, off
                 ALU.mult,
             )
 
-        def fetch_adv(t, a):
+        def plain_auction(t, b0, b1):
+            banks = slice(4 + 2 * t + b0, 4 + 2 * t + b1)
+            width = (b1 - b0) * BANK
+            ecpm2 = work.tile([P, width], F32, name="plain_ecpm2")
+            for b in range(b0, b1):
+                bank = 4 + 2 * t + b
+                nc.vector.scalar_tensor_tensor(
+                    ecpm2[:, (b - b0) * BANK : (b - b0 + 1) * BANK], half_tanh[:, bank, :], 1.0, logs[:, bank, :], ALU.add, ALU.mult
+                )
+            by_group = ecpm2[:].rearrange("p (v h e) -> p v h e", h=2, e=2)
+            pair_max = work.tile([P, width // D, 2], F32, name="plain_pair_max")
+            nc.vector.tensor_tensor(pair_max[:], by_group[:, :, 0, :], by_group[:, :, 1, :], ALU.max)
+            other_pair = work.tile([P, width // D, 2], F32, name="other_pair")
+            win2 = work.tile([P, width // D], F32, name="win2")
+            mid = width // D // 2
+            nc.vector.tensor_tensor(other_pair[:, :mid], by_group[:, :mid, ::-1, 0], by_group[:, :mid, ::-1, 1], ALU.add)
+            nc.vector.tensor_tensor(win2[:], pair_max[:, :, 0], pair_max[:, :, 1], ALU.max)
+            nc.vector.tensor_tensor(other_pair[:, mid:], by_group[:, mid:, ::-1, 0], by_group[:, mid:, ::-1, 1], ALU.add)
+            soft = half_tanh[:, banks, :].rearrange("p b c -> p (b c)")
+            nc.vector.tensor_tensor(
+                soft.rearrange("p (v d) -> p v d", d=D),
+                ecpm2[:].rearrange("p (v d) -> p v d", d=D),
+                win2[:].unsqueeze(2).to_broadcast([P, width // D, D]),
+                ALU.subtract,
+            )
+            others2 = logs[:, banks, :].rearrange("p b c -> p (b c)")
+            nc.vector.scalar_tensor_tensor(
+                others2.rearrange("p (u e) -> p u e", e=2),
+                other_pair[:].rearrange("p v h -> p (v h)").unsqueeze(2).to_broadcast([P, width // 2, 2]),
+                0.4,
+                ecpm2[:].rearrange("p (u e) -> p u e", e=2)[:, :, ::-1],
+                ALU.add,
+                ALU.add,
+            )
+            nc.scalar.activation(soft, soft, ACT.Tanh, scale=0.5)
+            nc.scalar.activation(soft, soft, ACT.Exp, scale=2.0)
+            price = shift_tanh[:, banks, :].rearrange("p b c -> p (b c)")
+            nc.vector.scalar_tensor_tensor(price, price, 1.6, others2, ALU.subtract, ALU.mult)
+            nc.vector.scalar_tensor_tensor(
+                pay[:, t, b0 * BANK : b1 * BANK], price, row_factor[:, t : t + 1], soft, ALU.mult, ALU.mult
+            )
+
+        def fetch_adv(t, a, TAIL):
             if t in ON_VECTOR:
                 nc.vector.tensor_copy(
                     out=pay_adv[:, t, a : a + TAIL], in_=scaled[t][:].indirect(adv_sb[:, a // 16 : (a + TAIL) // 16])
@@ -235,38 +315,41 @@ def tile_picked_yhqads_pay_p_kernel(tc, x_words, x_scales, w1, w2, unit, w3, off
                 scale=-0.4,
             )
 
-        made = {b: values(b) for b in ORDER}
         w3_bf = keep.tile([P, N, PACK], BF16, name="w3_bf", align_bytes=64)
         w3_codes = keep.tile([P, N], U32, name="w3_codes", align_bytes=64)
         w3_sc = keep.tile([P, N], U8, name="w3_sc", align_bytes=64)
         nc.vector.tensor_copy(out=w3_bf[:], in_=w3_raw[:].rearrange("p j n -> p n j"))
         nc.vector.quantize_mx(out=w3_codes[:].bitcast(FP8X4), scales=w3_sc[:], in_=w3_bf[:].rearrange("p n j -> p (n j)"))
 
-        for b in ORDER:
-            for t in range(PACK):
-                auction(b, t, *made[b])
+        for step in PLAN.split():
+            if step[0] == "A":
+                group_terms(int(step[1]))
+            elif step[0] == "N":
+                plain_auction(int(step[1]), int(step[2]), int(step[3]))
+            else:
+                turned_auction(int(step[1]), int(step[2]))
         scaled = {}
         for t in ON_VECTOR:
             scaled[t] = keep.tile([P, S], F32, name=f"scaled{t}")
             nc.vector.tensor_scalar(scaled[t][:], pay[:, t, :], -0.4, None, ALU.mult)
 
-        for a in range(0, S, TAIL):
+        for n, (a, TAIL) in enumerate(CHUNKS):
             cols = slice(a, a + TAIL)
             for t in range(PACK):
-                fetch_adv(t, a)
-            hid_bf = ring.tile([P, TAIL, PACK], BF16, name="hid_bf", align_bytes=64)
+                fetch_adv(t, a, TAIL)
+            hid_bf = last.tile([P, TAIL, PACK], BF16, name="hid_bf", align_bytes=64)
             nc.vector.tensor_tensor(
                 hid_bf[:].rearrange("p (c i) t -> p c t i", i=4),
                 pay[:, :, cols].rearrange("p t (c i) -> p c t i", i=4),
                 pay_adv[:, :, cols].rearrange("p t (c i) -> p c t i", i=4),
                 ALU.add,
             )
-            hid_codes = ring.tile([P, TAIL], U32, name="hid_codes", align_bytes=64)
-            hid_sc = ring.tile([P, TAIL], U8, name="hid_sc", align_bytes=64)
+            hid_codes = last.tile([P, TAIL], U32, name="hid_codes", align_bytes=64)
+            hid_sc = last.tile([P, TAIL], U8, name="hid_sc", align_bytes=64)
             nc.vector.quantize_mx(
                 out=hid_codes[:].bitcast(FP8X4), scales=hid_sc[:], in_=hid_bf[:].rearrange("p c t -> p (c t)")
             )
-            acc = psum.tile([P, BANK], F32, name=f"bank{a // TAIL}")
+            acc = psum.tile([P, BANK], F32, name=f"bank{n}")
             nc.tensor.matmul_mx(
                 out=acc[:, :TAIL],
                 lhsT=w3_codes[:].bitcast(FP8X4),
@@ -276,6 +359,6 @@ def tile_picked_yhqads_pay_p_kernel(tc, x_words, x_scales, w1, w2, unit, w3, off
                 start=True,
                 stop=True,
             )
-            result = ring.tile([P, TAIL], F32, name="result")
+            result = last.tile([P, TAIL], F32, name="result")
             nc.scalar.copy(out=result[:], in_=acc[:, :TAIL])
             nc.sync.dma_start(out=out[:, cols], in_=result[:])

import math
from contextlib import ExitStack

import concourse.mybir as mybir
from concourse.masks import make_identity

K, T, S, D, N, H = 1024, 2048, 1024, 4, 128, 512
FLOPS = 2 * (2 * K * H * S + H * N * S)

F32 = mybir.dt.float32
BF16 = mybir.dt.bfloat16
I32 = mybir.dt.int32
U32 = mybir.dt.uint32
U16 = mybir.dt.uint16
U8 = mybir.dt.uint8
FP8X4 = mybir.dt.float8_e4m3fn_x4
ALU = mybir.AluOpType
ACT = mybir.ActivationFunctionType

P = 128
PACK = 4
K_PASS = P * PACK
PASSES = K // K_PASS
BANK = 512
BLOCKS = S // BANK
CHUNKS = ((0, 256), (256, 256), (512, 256), (768, 128), (896, 128))
SOFTPLUS_CAP = 40.0
SHIFT = 0.5 * math.log(1.3 / 0.3)
EDGE = 16
PAIRED = (0, 1)
CUTS = 4
SHARE = 48
ON_VECTOR = ()
TURNED = 2
WIDE = TURNED * P
PLAN = "A0 A1 N002 U02 U12 N102 U03 U13"


def tile_picked_yhqads_pay_p_kernel(tc, x_words, x_scales, w1, w2, unit, w3, offs, adv, out):
    nc = tc.nc
    with ExitStack() as ctx:
        keep = ctx.enter_context(tc.tile_pool(name="keep", bufs=1))
        work = ctx.enter_context(tc.tile_pool(name="work", bufs=2))
        ring = ctx.enter_context(tc.tile_pool(name="ring", bufs=3))
        last = ctx.enter_context(tc.tile_pool(name="last", bufs=4))
        psum = ctx.enter_context(tc.psum_pool(name="psum", bufs=1))

        offs_sb = keep.tile([P, S // 16], U16, name="offs_sb")
        adv_sb = keep.tile([P, S // 16], U16, name="adv_sb")
        table_scales = keep.tile([P, T], U8, name="table_scales", align_bytes=64)
        scale_rows = keep.tile([P, T // 4], I32, name="scale_rows", align_bytes=64)
        table_words = [keep.tile([P, T], I32, name=f"table_words{o}", align_bytes=64) for o in range(PASSES)]
        w_raw = {}
        for nm in ("w2", "w1"):
            for o in range(PASSES):
                w_raw[nm, o] = keep.tile([P, PACK, H], F32, name=f"{nm}_raw{o}", align_bytes=64)
        w3_raw = keep.tile([P, PACK, N], F32, name="w3_raw", align_bytes=64)
        unit_sb = keep.tile([P, PACK], F32, name="unit_sb")

        def load_weight(nm, w, o):
            rows = w[o * K_PASS : (o + 1) * K_PASS, :]
            nc.sync.dma_start(out=w_raw[nm, o][:], in_=rows.rearrange("(p j) c -> p j c", j=PACK))

        def load_words(o):
            nc.sync.dma_start(out=table_words[o][:], in_=x_words[o].rearrange("p n t -> p (n t)").bitcast(I32))

        nc.vector.memset(table_scales[:].bitcast(I32), 0)
        nc.sync.dma_start(offs_sb[:], offs)
        for q in range(4):
            nc.sync.dma_start(
                out=scale_rows[32 * q : 32 * q + 4 * PASSES, :],
                in_=x_scales[:, 4 * q : 4 * q + 4, :].bitcast(I32),
            )
        load_weight("w2", w2, 0)
        load_words(0)
        load_words(1)
        load_weight("w2", w2, 1)
        load_weight("w1", w1, 0)
        load_weight("w1", w1, 1)
        nc.sync.dma_start(adv_sb[:], adv)
        nc.sync.dma_start(out=unit_sb[:], in_=unit.rearrange("(p t) o -> p (t o)", t=PACK))
        nc.sync.dma_start(out=w3_raw[:], in_=w3.rearrange("(p j) n -> p j n", j=PACK))

        ident = keep.tile([P, P], F32, name="ident")
        make_identity(nc, ident[:])
        picked_sc = keep.tile([P, S], U8, name="picked_sc", align_bytes=64)
        x_sc = keep.tile([P, BLOCKS, D, P], U8, name="x_sc", align_bytes=64)
        x_codes = {}
        w_codes = {}
        w_sc = {}
        w_bf = {}
        for key in w_raw:
            w_bf[key] = keep.tile([P, PACK, P, PACK], BF16, name=f"{key[0]}_bf{key[1]}", align_bytes=64)
            w_codes[key] = keep.tile([P, H], U32, name=f"{key[0]}_codes{key[1]}", align_bytes=64)
            w_sc[key] = keep.tile([P, H], U8, name=f"{key[0]}_sc{key[1]}", align_bytes=64)

        def gather_words(o, b):
            tag = "w2_bf1" if (o, b) == (1, 1) else f"x_codes{o}{b}"
            x_codes[o, b] = keep.tile([P, D, P], U32, name=f"x_codes{o}{b}", tag=tag, align_bytes=64)
            nc.vector.tensor_copy(
                out=x_codes[o, b][:].rearrange("p d v -> p v d"),
                in_=table_words[o][:].bitcast(U32).indirect(offs_sb[:, b * BANK // 16 : (b + 1) * BANK // 16]),
            )

        def round_weight(key, on_scalar):
            dst = w_bf[key][:].rearrange("p t m j -> p m j t")
            src = w_raw[key][:].rearrange("p j (m t) -> p m j t", t=PACK)
            if on_scalar > 0:
                nc.scalar.copy(out=dst[:, :on_scalar], in_=src[:, :on_scalar])
            if on_scalar == 0:
                for m in range(0, P, P // CUTS):
                    nc.vector.tensor_copy(out=dst[:, m : m + P // CUTS], in_=src[:, m : m + P // CUTS])
            elif on_scalar < P:
                nc.vector.tensor_copy(out=dst[:, on_scalar:], in_=src[:, on_scalar:])

        def quantize_weight(key):
            nc.vector.quantize_mx(
                out=w_codes[key][:].bitcast(FP8X4),
                scales=w_sc[key][:],
                in_=w_bf[key][:].rearrange("p t m j -> p (t m j)"),
            )

        def product(nm, bank):
            acc = psum.tile([P, BANK], F32, name=f"bank{bank}")
            if bank < 4:
                b, pair = divmod(bank, 2)
                for o in range(PASSES):
                    for e in range(2):
                        d = 2 * pair + e
                        nc.tensor.matmul_mx(
                            out=acc[:, e * WIDE : (e + 1) * WIDE],
                            lhsT=x_codes[o, b][:, d, :].bitcast(FP8X4),
                            lhsT_scale=x_sc[4 * o :, b, d, :],
                            rhs=w_codes[nm, o][:, H - WIDE :].bitcast(FP8X4),
                            rhs_scale=w_sc[nm, o][:, H - WIDE :],
                            start=(o == 0 and e == 0),
                            stop=(o == PASSES - 1 and e == 1),
                        )
                return acc[:].rearrange("p (v d) -> p v d", d=D)
            t, b = divmod(bank - 4, 2)
            rows = slice(t * P, (t + 1) * P)
            for o in range(PASSES):
                nc.tensor.matmul_mx(
                    out=acc[:],
                    lhsT=w_codes[nm, o][:, rows].bitcast(FP8X4),
                    lhsT_scale=w_sc[nm, o][:, rows],
                    rhs=x_codes[o, b][:].rearrange("p d v -> p (d v)").bitcast(FP8X4),
                    rhs_scale=x_sc[4 * o :, b].rearrange("p d v -> p (d v)"),
                    start=(o == 0),
                    stop=(o == PASSES - 1),
                )
            return acc[:].rearrange("p (d v) -> p v d", d=D)

        for q in range(4):
            live = slice(32 * q, 32 * q + 4 * PASSES)
            nc.vector.tensor_copy(out=table_scales[live, :].bitcast(I32), in_=scale_rows[live, :])

        def gather_scales(b):
            picked = picked_sc[:, b * BANK : (b + 1) * BANK]
            nc.vector.tensor_copy(out=picked, in_=table_scales[:].indirect(offs_sb[:, b * BANK // 16 : (b + 1) * BANK // 16]))
            nc.vector.tensor_copy(out=x_sc[:, b].rearrange("p d v -> p v d"), in_=picked.rearrange("p (v d) -> p v d", d=D))

        gather_scales(0)
        round_weight(("w2", 0), P)
        quantize_weight(("w2", 0))
        gather_words(0, 0)
        gather_words(1, 0)
        round_weight(("w2", 1), SHARE)
        quantize_weight(("w2", 1))
        gather_scales(1)
        gather_words(0, 1)
        gather_words(1, 1)

        logs = keep.tile([P, 8, BANK], F32, name="logs")
        half_tanh = keep.tile([P, 8, BANK], F32, name="half_tanh")
        shift_tanh = keep.tile([P, 8, BANK], F32, name="shift_tanh")
        pay = keep.tile([P, PACK, S], F32, name="pay")
        pay_adv = keep.tile([P, PACK, S], F32, name="pay_adv")
        row_factor = keep.tile([P, PACK], F32, name="row_factor")

        def as_bank(tile, bank):
            return tile[:, bank, :].rearrange("p (v d) -> p v d", d=D)

        yp = {}
        for bank in (0, 1, 4, 6, 2, 3, 5, 7):
            yp[bank] = product("w2", bank)
            nc.scalar.activation(as_bank(logs, bank), yp[bank], ACT.Exp)
        for piece in [logs[:, 0:2, EDGE:], logs[:, 4::2, EDGE:], logs[:, 2:4, EDGE:], logs[:, 5::2, EDGE:], logs[:, :, :EDGE]]:
            nc.vector.tensor_scalar(piece, piece, math.exp(SOFTPLUS_CAP), None, ALU.min)
        round_weight(("w1", 0), 0)
        quantize_weight(("w1", 0))
        round_weight(("w1", 1), 0)
        quantize_weight(("w1", 1))
        for n in range(0, 8, 2):
            nc.scalar.activation(logs[:, n : n + 2, :], logs[:, n : n + 2, :], ACT.Ln, bias=1.0)
        nc.vector.tensor_scalar(row_factor[:], unit_sb[:], -25.0 / 39.0, None, ALU.mult)
        for bank in range(8):
            nc.vector.tensor_tensor(as_bank(logs, bank), yp[bank], as_bank(logs, bank), ALU.max)
        for banks in ((0, 1, 2, 3), (4, 5), (6, 7)):
            ys = {bank: product("w1", bank) for bank in banks}
            for bank in banks:
                nc.scalar.activation(as_bank(half_tanh, bank), ys[bank], ACT.Tanh, scale=0.5)
            for bank in banks:
                nc.scalar.activation(as_bank(shift_tanh, bank), ys[bank], ACT.Tanh, scale=0.5, bias=SHIFT)

        terms = {}

        def group_terms(b):
            ecpm2 = work.tile([P, D, WIDE], F32, name="ecpm2")
            pair_max = work.tile([P, 2, WIDE], F32, name="pair_max")
            pair_sum = work.tile([P, 2, WIDE], F32, name="pair_sum")
            neg_win2 = work.tile([P, WIDE], F32, name="neg_win2")
            for pair in range(2):
                nc.vector.scalar_tensor_tensor(
                    ecpm2[:, 2 * pair : 2 * pair + 2, :].rearrange("p e c -> p (e c)"),
                    half_tanh[:, 2 * b + pair, :],
                    1.0,
                    logs[:, 2 * b + pair, :],
                    ALU.add,
                    ALU.mult,
                )
            nc.vector.tensor_tensor(pair_max[:], ecpm2[:, 0:2, :], ecpm2[:, 2:4, :], ALU.max)
            if b in PAIRED:
                nc.vector.scalar_tensor_tensor(pair_sum[:], ecpm2[:, 0::2, :], 0.4, ecpm2[:, 1::2, :], ALU.add, ALU.add)
            nc.vector.tensor_tensor(neg_win2[:], pair_max[:, 0, :], pair_max[:, 1, :], ALU.max)
            nc.vector.tensor_scalar(neg_win2[:], neg_win2[:], -1.0, None, ALU.mult)
            terms[b] = ecpm2, pair_sum, neg_win2

        turns = []

        def turned_sum(parts):
            acc = psum.tile([P, D, P], F32, name=f"bank{len(turns) % 8}")
            turns.append(acc)
            for d in range(D):
                for n, part in enumerate(parts[d]):
                    nc.tensor.matmul(
                        acc[:, d, :], part, ident[:], start=(n == 0), stop=(n == len(parts[d]) - 1), is_transpose=True
                    )
            return acc[:].rearrange("p d v -> p v d")

        def turned_auction(b, t):
            ecpm2, pair_sum, neg_win2 = terms[b]
            lo = (t - (PACK - TURNED)) * P
            rows = slice(lo, lo + P)
            shifted = shift_tanh[:, 2 * b : 2 * b + 2, :].rearrange("p a (e c) -> p (a e) c", e=2)
            others2 = turned_sum([[pair_sum[:, 1 - d // 2, rows], ecpm2[:, d ^ 1, rows]] for d in range(D)])
            gap2 = turned_sum([[neg_win2[:, rows], ecpm2[:, d, rows]] for d in range(D)])
            shift_turned = turned_sum([[shifted[:, d, rows]] for d in range(D)])
            soft = ring.tile([P, P, D], F32, name="soft")
            nc.scalar.activation(soft[:], gap2, ACT.Tanh, scale=0.5)
            nc.scalar.activation(soft[:], soft[:], ACT.Exp, scale=2.0)
            price = ring.tile([P, P, D], F32, name="price")
            nc.vector.scalar_tensor_tensor(price[:], others2, row_factor[:, t : t + 1], soft[:], ALU.mult, ALU.mult)
            nc.vector.scalar_tensor_tensor(
                pay[:, t, b * BANK : (b + 1) * BANK].rearrange("p (v d) -> p v d", d=D),
                shift_turned,
                1.6,
                price[:],
                ALU.subtract,
                ALU.mult,
            )

        def plain_auction(t, b0, b1):
            banks = slice(4 + 2 * t + b0, 4 + 2 * t + b1)
            width = (b1 - b0) * BANK
            ecpm2 = work.tile([P, width], F32, name="plain_ecpm2")
            for b in range(b0, b1):
                bank = 4 + 2 * t + b
                nc.vector.scalar_tensor_tensor(
                    ecpm2[:, (b - b0) * BANK : (b - b0 + 1) * BANK], half_tanh[:, bank, :], 1.0, logs[:, bank, :], ALU.add, ALU.mult
                )
            by_group = ecpm2[:].rearrange("p (v h e) -> p v h e", h=2, e=2)
            pair_max = work.tile([P, width // D, 2], F32, name="plain_pair_max")
            nc.vector.tensor_tensor(pair_max[:], by_group[:, :, 0, :], by_group[:, :, 1, :], ALU.max)
            other_pair = work.tile([P, width // D, 2], F32, name="other_pair")
            win2 = work.tile([P, width // D], F32, name="win2")
            mid = width // D // 2
            nc.vector.tensor_tensor(other_pair[:, :mid], by_group[:, :mid, ::-1, 0], by_group[:, :mid, ::-1, 1], ALU.add)
            nc.vector.tensor_tensor(win2[:], pair_max[:, :, 0], pair_max[:, :, 1], ALU.max)
            nc.vector.tensor_tensor(other_pair[:, mid:], by_group[:, mid:, ::-1, 0], by_group[:, mid:, ::-1, 1], ALU.add)
            soft = half_tanh[:, banks, :].rearrange("p b c -> p (b c)")
            nc.vector.tensor_tensor(
                soft.rearrange("p (v d) -> p v d", d=D),
                ecpm2[:].rearrange("p (v d) -> p v d", d=D),
                win2[:].unsqueeze(2).to_broadcast([P, width // D, D]),
                ALU.subtract,
            )
            others2 = logs[:, banks, :].rearrange("p b c -> p (b c)")
            nc.vector.scalar_tensor_tensor(
                others2.rearrange("p (u e) -> p u e", e=2),
                other_pair[:].rearrange("p v h -> p (v h)").unsqueeze(2).to_broadcast([P, width // 2, 2]),
                0.4,
                ecpm2[:].rearrange("p (u e) -> p u e", e=2)[:, :, ::-1],
                ALU.add,
                ALU.add,
            )
            nc.scalar.activation(soft, soft, ACT.Tanh, scale=0.5)
            nc.scalar.activation(soft, soft, ACT.Exp, scale=2.0)
            price = shift_tanh[:, banks, :].rearrange("p b c -> p (b c)")
            nc.vector.scalar_tensor_tensor(price, price, 1.6, others2, ALU.subtract, ALU.mult)
            nc.vector.scalar_tensor_tensor(
                pay[:, t, b0 * BANK : b1 * BANK], price, row_factor[:, t : t + 1], soft, ALU.mult, ALU.mult
            )

        def fetch_adv(t, a, TAIL):
            if t in ON_VECTOR:
                nc.vector.tensor_copy(
                    out=pay_adv[:, t, a : a + TAIL], in_=scaled[t][:].indirect(adv_sb[:, a // 16 : (a + TAIL) // 16])
                )
                return
            nc.scalar.activation(
                pay_adv[:, t, a : a + TAIL],
                pay[:, t, :].indirect(adv_sb[:, a // 16 : (a + TAIL) // 16]),
                ACT.Copy,
                scale=-0.4,
            )

        w3_bf = keep.tile([P, N, PACK], BF16, name="w3_bf", align_bytes=64)
        w3_codes = keep.tile([P, N], U32, name="w3_codes", align_bytes=64)
        w3_sc = keep.tile([P, N], U8, name="w3_sc", align_bytes=64)
        nc.vector.tensor_copy(out=w3_bf[:], in_=w3_raw[:].rearrange("p j n -> p n j"))
        nc.vector.quantize_mx(out=w3_codes[:].bitcast(FP8X4), scales=w3_sc[:], in_=w3_bf[:].rearrange("p n j -> p (n j)"))

        for step in PLAN.split():
            if step[0] == "A":
                group_terms(int(step[1]))
            elif step[0] == "N":
                plain_auction(int(step[1]), int(step[2]), int(step[3]))
            else:
                turned_auction(int(step[1]), int(step[2]))
        scaled = {}
        for t in ON_VECTOR:
            scaled[t] = keep.tile([P, S], F32, name=f"scaled{t}")
            nc.vector.tensor_scalar(scaled[t][:], pay[:, t, :], -0.4, None, ALU.mult)

        for n, (a, TAIL) in enumerate(CHUNKS):
            cols = slice(a, a + TAIL)
            for t in range(PACK):
                fetch_adv(t, a, TAIL)
            hid_bf = last.tile([P, TAIL, PACK], BF16, name="hid_bf", align_bytes=64)
            nc.vector.tensor_tensor(
                hid_bf[:].rearrange("p (c i) t -> p c t i", i=4),
                pay[:, :, cols].rearrange("p t (c i) -> p c t i", i=4),
                pay_adv[:, :, cols].rearrange("p t (c i) -> p c t i", i=4),
                ALU.add,
            )
            hid_codes = last.tile([P, TAIL], U32, name="hid_codes", align_bytes=64)
            hid_sc = last.tile([P, TAIL], U8, name="hid_sc", align_bytes=64)
            nc.vector.quantize_mx(
                out=hid_codes[:].bitcast(FP8X4), scales=hid_sc[:], in_=hid_bf[:].rearrange("p c t -> p (c t)")
            )
            acc = psum.tile([P, BANK], F32, name=f"bank{n}")
            nc.tensor.matmul_mx(
                out=acc[:, :TAIL],
                lhsT=w3_codes[:].bitcast(FP8X4),
                lhsT_scale=w3_sc[:],
                rhs=hid_codes[:].bitcast(FP8X4),
                rhs_scale=hid_sc[:],
                start=True,
                stop=True,
            )
            result = last.tile([P, TAIL], F32, name="result")
            nc.scalar.copy(out=result[:], in_=acc[:, :TAIL])
            nc.sync.dma_start(out=out[:, cols], in_=result[:])
